import numpy as np
import ml_dtypes


def mxq(x, axis, fmt="e4m3"):
    dtype, down = {"e4m3": (ml_dtypes.float8_e4m3fn, 7), "e5m2": (ml_dtypes.float8_e5m2, 14)}[fmt]
    v = np.moveaxis(np.asarray(x, np.float32).astype(ml_dtypes.bfloat16).astype(np.float64), axis, -1)
    blocks = v.reshape(v.shape[:-1] + (-1, 32))
    amax = np.abs(blocks).max(-1, keepdims=True)
    byte = np.maximum(np.where(amax > 0, np.frexp(amax)[1] - 1 + 127, 0) - down, 1)
    scale = np.exp2(byte - 127.0)
    codes = (blocks / scale).astype(np.float32).astype(dtype).astype(np.float64)
    return np.moveaxis((codes * scale).reshape(v.shape), -1, axis)


WIDE = False


def mx_kscale(k):
    if not WIDE:
        return np.ones(k)
    levels = np.array([10, -10, 5, -5, 0])
    if k % 512:
        return np.exp2(np.random.permutation(np.resize(levels, k // 32))).repeat(32)
    a = np.empty((k // 512, 16))
    for p in range(k // 512):
        a[p, :8] = np.random.permutation(np.resize(levels, 8))
        for g in range(8):
            far = levels[np.abs(levels - a[p, g]) >= 10]
            a[p, g + 8] = far[np.random.randint(len(far))]
    return np.exp2(a.ravel()).repeat(32)


def f64(x):
    return np.asarray(x).astype(np.float64)


def striped(idx):
    return np.tile(idx.reshape(-1, 16).T, (8, 1)).astype(np.uint16)


def unstriped(offs):
    return offs[:16].T.reshape(-1).astype(np.int64)


def striped8(idx):
    return np.concatenate([x.reshape(-1, 16).T for x in idx]).astype(np.uint16)


def runs(offs, k):
    lists = np.stack([offs[16 * r : 16 * r + 16].T.reshape(-1) for r in range(8)]).astype(np.int64)
    return lists[np.arange(k) % 512 // 64]


def pack_weight(w):
    k, n = w.shape
    w = f64(np.asarray(w, np.float32).astype(ml_dtypes.bfloat16)).reshape(k // 32, 32, n)
    amax = np.abs(w).max(1)
    byte = np.clip(np.where(amax > 0, np.frexp(amax)[1] - 1 + 127 - 7, 1), 1, 254)
    scaled = (w * np.exp2(127.0 - byte)[:, None, :]).reshape(k, n).astype(np.float32)
    words = np.ascontiguousarray(scaled.reshape(k // 512, 128, 4, n).transpose(0, 1, 3, 2)).astype(ml_dtypes.float8_e4m3fn).view(np.uint8)
    return words, np.ascontiguousarray(byte.astype(np.uint8).reshape(k // 512, 16, n))


def unpack_weight(words, scales):
    g, p, n, _ = words.shape
    vals = np.ascontiguousarray(words).view(ml_dtypes.float8_e4m3fn).astype(np.float64) * np.repeat(np.exp2(scales.astype(np.float64) - 127.0), 8, axis=1)[..., None]
    return vals.transpose(0, 1, 3, 2).reshape(g * 512, n)


E2M1 = np.array([0.0, 0.5, 1.0, 1.5, 2.0, 3.0, 4.0, 6.0, -0.0, -0.5, -1.0, -1.5, -2.0, -3.0, -4.0, -6.0])


def pack_fp4(w):
    k, n = w.shape
    w = f64(np.asarray(w, np.float32).astype(ml_dtypes.bfloat16)).reshape(k // 32, 32, n)
    amax = np.abs(w).max(1)
    mant, ex = np.frexp(amax / 6.0)
    byte = np.clip(np.where(amax > 0, np.where(mant > 0.5, ex, ex - 1) + 127, 1), 1, 254)
    scaled = (w * np.exp2(127.0 - byte)[:, None, :]).reshape(k, n).astype(np.float32)
    c = np.ascontiguousarray(scaled.reshape(k // 512, 128, 4, n).transpose(0, 1, 3, 2)).astype(ml_dtypes.float4_e2m1fn).view(np.uint8) & 0xF
    words = (c[..., 0::2] | (c[..., 1::2] << 4)).reshape(k // 512, 128, 2 * n)
    return np.ascontiguousarray(words), np.ascontiguousarray(byte.astype(np.uint8).reshape(k // 512, 16, n))


def unpack_fp4(words, scales):
    g, _, n = scales.shape
    words = np.ascontiguousarray(words).reshape(g, 128, n, 2)
    nib = np.empty((g, 128, n, 4), np.uint8)
    nib[..., 0::2] = words & 0xF
    nib[..., 1::2] = words >> 4
    vals = E2M1[nib] * np.repeat(np.exp2(scales.astype(np.float64) - 127.0), 8, axis=1)[..., None]
    return vals.transpose(0, 1, 3, 2).reshape(g * 512, n)


def sigmoid(v):
    return 1.0 / (1.0 + np.exp(-np.maximum(v, -700.0)))

def planes(y):
    n, m = y.shape
    v = y.astype(np.float32).astype(ml_dtypes.bfloat16).astype(np.float64).reshape(n // 32, 32, m)
    top = np.abs(v).max(1)
    byte = np.clip(np.where(top > 0, np.frexp(top)[1] - 1 + 127 - 7, 1), 1, 254)
    codes = (v * np.exp2(127.0 - byte)[:, None, :]).reshape(n, m).astype(np.float32).astype(ml_dtypes.float8_e4m3fn).view(np.uint8)
    words = codes.reshape(n // 512, 128, 4, m).transpose(0, 1, 3, 2)
    return np.ascontiguousarray(words), np.ascontiguousarray(byte.astype(np.uint8).reshape(n // 512, 16, m))


K, T, S, V, G, H, J = 512, 1024, 512, 512, 2048, 512, 512


def setup_inputs():
    n = np.random.standard_normal
    s = mx_kscale(K)[:, None]
    u = mx_kscale(S)
    packed_xT = pack_weight(n((K, T)) * s)
    packed_dT = pack_weight(n((K, G)) / s)
    packed_w1 = pack_fp4(n((K, H)) / np.sqrt(K) / s)
    return {
        "x_words": packed_xT[0],
        "x_scales": packed_xT[1],
        "d_words": packed_dT[0],
        "d_scales": packed_dT[1],
        "w1_words": packed_w1[0],
        "w1_scales": packed_w1[1],
        "tab": n((H, J)).astype(np.float32),
        "ga": (np.random.uniform(0.5, 1.5, (H, 1)) * u[:, None]).astype(np.float32),
        "gb": (np.random.uniform(0.5, 1.5, (H, 1)) / u[:, None]).astype(np.float32),
        "tab2": np.random.uniform(0.4, 1.4, (S, J)).astype(np.float32),
        "offs": striped(np.random.permutation(T)[:S]),
        "k1": striped8(np.random.randint(0, G, (8, H))),
        "two": striped(np.random.permutation(T)[:V]),
        "n1": striped8(np.stack([np.random.permutation(S) for _ in range(8)])),
        "n2": striped8(np.stack([np.random.permutation(S) for _ in range(8)])),
        "n3": striped8(np.random.randint(0, J, (8, V))),
        "n4": striped8(np.stack([np.random.permutation(V) for _ in range(8)])),
        "n5": striped8(np.random.randint(0, J, (8, V))),
        "n6": striped8(np.stack([np.random.permutation(V) for _ in range(8)])),
    }


def reference(x_words, x_scales, d_words, d_scales, w1_words, w1_scales, tab, ga, gb, tab2, offs, k1, two, n1, n2, n3, n4, n5, n6):
    d_k1 = unpack_weight(d_words, d_scales)[np.arange(K)[:, None], runs(k1, K)]
    xq = unpack_weight(x_words, x_scales)[:, unstriped(offs)]
    a = 0.0625 * (d_k1.T @ xq)
    st = a[np.arange(H)[:, None], runs(n1, H)] - a
    z = f64(ga) * (a * (sigmoid(st[np.arange(H)[:, None], runs(n2, H)])))
    x_two = unpack_weight(x_words, x_scales)[:, unstriped(two)]
    b = unpack_fp4(w1_words, w1_scales).T @ x_two
    z2 = f64(gb) * (np.maximum(b + f64(tab)[np.arange(H)[:, None], runs(n3, H)], b[np.arange(H)[:, None], runs(n4, H)]))
    s = 0.0625 * ((mxq(z, 0, "e4m3").T @ mxq(z2, 0, "e4m3")))
    out_0 = s * (f64(tab2)[np.arange(S)[:, None], runs(n5, S)]) - (0.5 * (s[np.arange(S)[:, None], runs(n6, S)]))
    return (out_0,) + planes(out_0)

from contextlib import ExitStack

import concourse.mybir as mybir
from concourse.masks import make_identity

F32 = mybir.dt.float32
BF16 = mybir.dt.bfloat16
I32 = mybir.dt.int32
U32 = mybir.dt.uint32
U16 = mybir.dt.uint16
U8 = mybir.dt.uint8
FP8X4 = mybir.dt.float8_e4m3fn_x4
FP4X4 = mybir.dt.float4_e2m1fn_x4
ALU = mybir.AluOpType
ACT = mybir.ActivationFunctionType

P = 128
PACK = 4
N = 512
T = 1024
G = 2048
WINDOW = 2 * N
HALF = N // 2
FLOPS = 3 * 2 * N * N * N


def tile_picked_ckqhopdkindkindg_none_po_kernel(
    tc, x_words, x_scales, d_words, d_scales, w1_words, w1_scales, tab, ga, gb, tab2,
    offs, k1, two, n1, n2, n3, n4, n5, n6, out_0, out_1, out_2,
):
    nc = tc.nc
    with ExitStack() as ctx:
        keep = ctx.enter_context(tc.tile_pool(name="keep", bufs=1))
        psum = ctx.enter_context(tc.psum_pool(name="psum", bufs=1))

        def load_list(name, src):
            tile = keep.tile([P, N // 16], U16, name=name)
            nc.sync.dma_start(tile[:], src)
            return tile

        def load_scale_rows(name, src, width):
            tile = keep.tile([P, width], U8, name=name, align_bytes=64)
            rows = src[0].bitcast(I32).unsqueeze(1).to_broadcast([16, 8, width // 4])
            nc.sync.dma_start(tile[:].bitcast(I32), rows)
            return tile

        def load_words(name, src, width):
            tile = keep.tile([P, width], I32, name=name, align_bytes=64)
            nc.sync.dma_start(tile[:], src.bitcast(I32))
            return tile

        def windows(name, width):
            return [keep.tile([P, width], F32, name=name + str(t)) for t in range(PACK)]

        out_scales = keep.tile([P, N], U8, align_bytes=64)
        z_scales = keep.tile([P, N], U8, align_bytes=64)
        z2_scales = keep.tile([P, N], U8, align_bytes=64)

        warm = keep.tile([P, 2], F32)
        nc.gpsimd.memset(warm[:, 0:1], 0.0)
        nc.scalar.activation(warm[:, 1:2], warm[:, 0:1], ACT.Sigmoid)

        k1_sb = load_list("k1_sb", k1)
        d_rows = load_scale_rows("d_rows", d_scales, G)
        offs_sb = load_list("offs_sb", offs)
        x_rows = load_scale_rows("x_rows", x_scales, T)
        two_sb = load_list("two_sb", two)
        w1_rows = load_scale_rows("w1_rows", w1_scales, N)
        d_table = load_words("d_table", d_words[0].rearrange("p n r -> p (n r)"), G)
        x_table = load_words("x_table", x_words[0].rearrange("p n r -> p (n r)"), T)
        n1_sb = load_list("n1_sb", n1)
        n3_sb = load_list("n3_sb", n3)
        n4_sb = load_list("n4_sb", n4)
        n2_sb = load_list("n2_sb", n2)
        n5_sb = load_list("n5_sb", n5)
        n6_sb = load_list("n6_sb", n6)
        w1_raw = load_words("w1_raw", w1_words[0], N // 2)
        tab_raw = [keep.tile([P, N], F32, name="tab_raw" + str(t)) for t in range(PACK)]
        for t in range(PACK):
            nc.sync.dma_start(tab_raw[t][:], tab.rearrange("(b t e) n -> t b e n", t=PACK, e=8)[t])

        planes = keep.tile([P, 4, N], U8, align_bytes=64)
        nc.vector.memset(planes[:].rearrange("p a n -> p (a n)").bitcast(I32), 0)
        gain_rows = keep.tile([P, P], F32)
        identity = keep.tile([P, P], F32)
        nc.gpsimd.memset(gain_rows[:], 0.0)
        for first, gain in ((0, gb), (PACK, ga)):
            nc.gpsimd.dma_start(gain_rows[first:first + PACK, :], gain.rearrange("(b t e) o -> t b (e o)", t=PACK, e=8))
        make_identity(nc, identity[:])
        gain_bank = psum.tile([P, P], F32, name="gain_bank", tag="second0")
        nc.tensor.transpose(gain_bank[:], gain_rows[:], identity[:])
        gb_abs = keep.tile([P, PACK], F32)
        nc.scalar.activation(gb_abs[:], gain_bank[:, :PACK], ACT.Abs)
        gains = keep.tile([P, 2 * PACK], F32)
        nc.scalar.copy(gains[:], gain_bank[:, :2 * PACK])
        gb_sb = gains[:, :PACK]
        ga_sb = gains[:, PACK:]
        step = keep.tile([P, PACK], F32)
        sign = keep.tile([P, PACK], F32)
        ga_signed = keep.tile([P, PACK], F32)
        a_gain = keep.tile([P, PACK], F32)
        nc.gpsimd.tensor_scalar(step[:], gb_sb, 0.0, 2.0, ALU.is_ge, ALU.mult)
        nc.gpsimd.tensor_scalar(sign[:], step[:], 1.0, -1.0, ALU.mult, ALU.add)
        nc.gpsimd.tensor_tensor(ga_signed[:], ga_sb, sign[:], ALU.mult)
        nc.gpsimd.tensor_scalar(a_gain[:], ga_signed[:], 0.0625, 0.0, ALU.mult, ALU.add)

        d_picked = keep.tile([P, N], U8, align_bytes=64, tag="d_picks")
        x_picked = keep.tile([P, 2, N], U8, align_bytes=64, tag="x_picks")
        staged = keep.tile([P, 4, N], U8, align_bytes=64, tag="late")
        nc.vector.tensor_copy(d_picked[:], d_rows[:].indirect(k1_sb[:]))
        nc.vector.tensor_copy(x_picked[:, 1, :], x_rows[:].indirect(offs_sb[:]))
        nc.vector.tensor_copy(x_picked[:, 0, :], x_rows[:].indirect(two_sb[:]))
        def deal(dst, src):
            words = src.bitcast(I32)
            run = words.shape[1] * 8 // N
            nc.vector.tensor_copy(
                dst.bitcast(I32).rearrange("p (t b e) -> p t b e", t=PACK, e=run),
                words.rearrange("p (b t e) -> p t b e", t=PACK, e=run))

        deal(staged[:, 1, :], w1_rows[:])
        deal(staged[:, 0, :], d_picked[:])
        nc.vector.tensor_copy(
            staged[:, 2:4, :].rearrange("p a n -> p (a n)").bitcast(I32),
            x_picked[:].rearrange("p a n -> p (a n)").bitcast(I32))
        for r in range(4):
            nc.scalar.dma_start(
                planes[:].rearrange("p a n -> p (a n)").bitcast(I32)[r:P:32, :],
                staged[:].rearrange("p a n -> p (a n)").bitcast(I32)[8 * r:P:32, :])
        tab2_raw = keep.tile([P, PACK, N], F32, align_bytes=64, tag="late")
        nc.sync.dma_start(tab2_raw[:], tab2.rearrange("(p t) n -> p t n", t=PACK))
        d_plane, w1_plane, two_plane, offs_plane = (planes[:, a, :] for a in range(4))

        two_codes = keep.tile([P, N], U32, align_bytes=64)
        offs_codes = keep.tile([P, N], U32, align_bytes=64, tag="x_picks")
        d_gathered = keep.tile([P, N], U32, align_bytes=64, tag="d_picks")
        d_codes = keep.tile([P, PACK, P], U32, align_bytes=64)
        w1_codes = keep.tile([P, PACK, 2 * P], U8, align_bytes=64)
        nc.vector.tensor_copy(d_gathered[:], d_table[:].bitcast(U32).indirect(k1_sb[:]))
        nc.vector.tensor_copy(offs_codes[:], x_table[:].bitcast(U32).indirect(offs_sb[:]))
        deal(d_codes[:].rearrange("p t m -> p (t m)"), d_gathered[:])
        nc.vector.tensor_copy(two_codes[:], x_table[:].bitcast(U32).indirect(two_sb[:]))
        deal(w1_codes[:].rearrange("p t m -> p (t m)"), w1_raw[:])

        tab_win, b_win, a_win, st_win = (windows(n, WINDOW) for n in ("tab_win", "b_win", "a_win", "st_win"))
        tab2_win, s_win = (windows(n, N) for n in ("tab2_win", "s_win"))
        for t in range(PACK):
            nc.scalar.activation(tab_win[t][:, :N], tab_raw[t][:], ACT.Copy, scale=gb_abs[:, t:t + 1])

        a_plain = keep.tile([P, PACK, N], F32)
        a_gained = keep.tile([P, PACK, N], F32)
        a_banks = []
        for t in range(PACK):
            bank = psum.tile([P, N], F32, name="a_bank", tag="first" + str(t))
            nc.tensor.matmul_mx(
                bank[:], lhsT=d_codes[:, t, :].bitcast(FP8X4), lhsT_scale=d_plane[:, t * P:(t + 1) * P],
                rhs=offs_codes[:].bitcast(FP8X4), rhs_scale=offs_plane, start=True, stop=True)
            nc.scalar.activation(a_win[t][:, :N], bank[:], ACT.Copy, scale=0.0625)
            nc.scalar.activation(a_plain[:, t, :], bank[:], ACT.Copy, scale=0.0625)
            nc.vector.tensor_tensor(st_win[t][:, :N], a_win[t][:].indirect(n1_sb[:]), a_plain[:, t, :], ALU.subtract)
            a_banks.append(bank)

        left = keep.tile([P, PACK, N], F32)
        right = keep.tile([P, PACK, N], F32)
        gate = keep.tile([P, PACK, N], F32)
        for t in range(PACK):
            bank = psum.tile([P, N], F32, name="b_bank", tag="second" + str(t))
            nc.tensor.matmul_mx(
                bank[:], lhsT=w1_codes[:, t, :].bitcast(FP4X4), lhsT_scale=w1_plane[:, t * P:(t + 1) * P],
                rhs=two_codes[:].bitcast(FP8X4), rhs_scale=two_plane, start=True, stop=True)
            nc.scalar.activation(b_win[t][:, :N], bank[:], ACT.Copy, scale=gb_abs[:, t:t + 1])
            nc.vector.tensor_tensor(left[:, t, :], tab_win[t][:].indirect(n3_sb[:]), b_win[t][:, :N], ALU.add)
            nc.vector.tensor_copy(right[:, t, :], b_win[t][:].indirect(n4_sb[:]))

        for t in range(PACK):
            nc.scalar.activation(gate[:, t, :], st_win[t][:].indirect(n2_sb[:]), ACT.Sigmoid)
        for t in range(PACK):
            nc.scalar.activation(a_gained[:, t, :], a_banks[t][:], ACT.Copy, scale=a_gain[:, t:t + 1])
        for t in range(PACK):
            nc.scalar.activation(tab2_win[t][:, :N], tab2_raw[:, t, :], ACT.Copy, scale=-2.0)

        z_grouped = keep.tile([P, PACK * N], BF16, align_bytes=64)
        z_codes = keep.tile([P, N], U32, align_bytes=64)
        nc.vector.tensor_tensor(
            z_grouped[:].rearrange("p (u m t) -> p m t u", u=PACK, t=PACK),
            a_gained[:].rearrange("p t (m u) -> p m t u", u=PACK),
            gate[:].rearrange("p t (m u) -> p m t u", u=PACK), ALU.mult)
        z2_grouped = keep.tile([P, 2, PACK * HALF], BF16, align_bytes=64)
        z2_codes = keep.tile([P, N], U32, align_bytes=64)

        def larger(h):
            cols = slice(h * HALF, (h + 1) * HALF)
            nc.vector.tensor_tensor(
                z2_grouped[:, h, :].rearrange("p (c i t) -> p c t i", i=4, t=PACK),
                left[:, :, cols].rearrange("p t (c i) -> p c t i", i=4),
                right[:, :, cols].rearrange("p t (c i) -> p c t i", i=4), ALU.max)

        s_banks = [psum.tile([P, N], F32, name="s_bank", tag="second" + str(t)) for t in range(PACK)]

        def third_product(h):
            cols = slice(h * HALF, (h + 1) * HALF)
            nc.vector.quantize_mx(z2_codes[:, cols].bitcast(FP8X4), z2_scales[:, cols], z2_grouped[:, h, :])
            for t in range(PACK):
                nc.tensor.matmul_mx(
                    s_banks[t][:, cols], lhsT=z_codes[:, t * P:(t + 1) * P].bitcast(FP8X4),
                    lhsT_scale=z_scales[:, t * P:(t + 1) * P],
                    rhs=z2_codes[:, cols].bitcast(FP8X4), rhs_scale=z2_scales[:, cols], start=True, stop=True)
                nc.scalar.activation(s_win[t][:, cols], s_banks[t][:, cols], ACT.Copy, scale=-0.03125)

        scaled = keep.tile([P, PACK, N], F32)
        result = keep.tile([P, PACK, N], F32)

        def times_table(h, t):
            cols = slice(h * HALF, (h + 1) * HALF)
            entries = slice(h * HALF // 16, (h + 1) * HALF // 16)
            nc.vector.tensor_tensor(
                scaled[:, t, cols], tab2_win[t][:].indirect(n5_sb[:, entries]), s_win[t][:, cols], ALU.mult)

        larger(0)
        nc.vector.quantize_mx(z_codes[:].bitcast(FP8X4), z_scales[:], z_grouped[:])
        third_product(0)
        larger(1)
        times_table(0, 0)
        third_product(1)
        for t in range(1, PACK):
            times_table(0, t)
        for t in range(PACK):
            times_table(1, t)

        out_grouped = keep.tile([P, PACK * N], BF16, align_bytes=64)
        out_codes = keep.tile([P, N], U32, align_bytes=64)
        out_rows = out_0.rearrange("(p t) n -> p t n", t=PACK)
        out_words = out_1[0].rearrange("p n r -> p (n r)").bitcast(I32)
        pieces = ((0, 256), (256, 384), (384, 512))

        def quantise_out(lo, hi):
            nc.vector.quantize_mx(out_codes[:, lo:hi].bitcast(FP8X4), out_scales[:, lo:hi], out_grouped[:, PACK * lo:PACK * hi])
            nc.sync.dma_start(out_words[:, lo:hi], out_codes[:, lo:hi].bitcast(I32))

        for k, (lo, hi) in enumerate(pieces):
            for t in range(PACK):
                nc.vector.tensor_tensor(
                    result[:, t, lo:hi], s_win[t][:].indirect(n6_sb[:, lo // 16:hi // 16]), scaled[:, t, lo:hi], ALU.add)
            nc.sync.dma_start(out_rows[:, :, lo:hi], result[:, :, lo:hi])
            dst = out_grouped[:, PACK * lo:PACK * hi].rearrange("p (c i t) -> p c t i", i=4, t=PACK)
            src = result[:, :, lo:hi].rearrange("p t (c i) -> p c t i", i=4)
            if k < len(pieces) - 1:
                nc.scalar.copy(dst, src)
            else:
                nc.vector.tensor_copy(dst, src)
            if k > 0:
                quantise_out(*pieces[k - 1])
        quantise_out(*pieces[-1])
        for q in range(4):
            queue = nc.scalar if q % 2 else nc.sync
            queue.dma_start(out_2[0, 4 * q:4 * q + 4, :].bitcast(I32), out_scales[32 * q:32 * q + 4, :].bitcast(I32))
